import numpy as np, ml_dtypes
CORES = [48,51,52,55]
N = 4
import mx_ref
BF = ml_dtypes.bfloat16
def entries(a):
    return np.ascontiguousarray(a.T).reshape(-1)
def table(e):
    return np.ascontiguousarray(np.reshape(e, (-1, 16)).T).astype(np.int32)
def cols(t, e):
    v = np.concatenate([t.reshape(128, -1, 4), np.zeros((128, 1, 4), BF)], axis=1)
    return np.ascontiguousarray(v[:, e]).reshape(128, -1)
def f(rng, *shape):
    return mx_ref.flush((rng.standard_normal(shape, dtype=np.float32) * np.exp2(rng.integers(-2, 3, shape[:-1] + (1,)))).astype(BF))
def wide(rng, *shape, cols=0):
    v = rng.standard_normal(shape, dtype=np.float32) * np.exp2(rng.integers(-12, 13, shape)).astype(np.float32)
    if cols: v *= np.repeat(np.exp2(rng.integers(-cols, cols + 1, shape[:-2] + (1, shape[-1] // 4))) * (rng.random(shape[:-2] + (1, shape[-1] // 4)) > 0.0625), 4, axis=-1).astype(np.float32)
    return mx_ref.flush(v.astype(BF))
T, S, CAPP, CL, K, O = 512, 512, 160, 160, 2048, 2
H = 65536 // (N * K)
def counts(rng, tot, cap, lead=None, least=2):
    n = np.full(N, least)
    if lead is not None:
        for i in range(N):
            q = (lead + i) % N; n[q] += min(cap - n[q], tot - n.sum())
    while n.sum() < tot:
        q = rng.integers(0, N)
        if n[q] < cap: n[q] += 1
    return n
def lists(rng, full=False, hot=False, other=False, few=False):
    a, b = rng.integers(1, N, 2); z = rng.integers(0, N); least = 0 if full else 2
    n = np.stack([counts(rng, T, CAPP, (r + a) % N if full or other else z if hot else None, least) for r in range(N)])
    part, pool = [], []
    for q in range(N):
        c = n[:, q].sum(); p = rng.permutation(K)[:c]
        key = q + N * (p + K * rng.integers(0, H, c))
        part.append(np.split(key, np.cumsum(n[:, q])[:-1])); pool.append(rng.choice(key, 1) if few else key)
    has = [np.concatenate([part[q][r] for q in range(N)]) for r in range(N)]
    ky, lk = [], []
    for r in range(N):
        ky.append(table(rng.permutation(has[r])))
        if other:
            s = (r + a) % N; e = rng.permutation(has[s])[:S]; m = np.bincount(e & (N - 1), minlength=N); e = [e]
            for q in ((s + a) % N, (s + a + 1) % N):
                more = rng.permutation(np.setdiff1d(pool[q], part[q][s]))[:CL - m[q]]
                e.append(more); m[q] += len(more)
            while m.sum() < S:
                q = rng.integers(0, N)
                if m[q] < CL: m[q] += 1; e.append(rng.choice(part[q][s], 1))
            u = np.unique(np.concatenate(e)); lead = part[(s + a) % N][s]
            assert len(lead) == CAPP and np.isin(lead, u).all()
            assert any(q != r and m[q] == CL and ((u & (N - 1)) == q).sum() == CL for q in range(N))
        else:
            m = counts(rng, S, CL, (r + b) % N if full else z if hot else None, least)
            e = [rng.choice(pool[q], m[q]) for q in range(N)]
        lk.append(table(rng.permutation(np.concatenate(e))))
    return {"ky": np.stack(ky), "lk": np.stack(lk)}
def setup_inputs(rng):
    d = lists(rng)
    return {"x": f(rng, N, 128, 4 * T), "ky": d["ky"], "lk": d["lk"], "w": f(rng, N, 128, 512 * O)}
def setup_inputs_full(rng):
    return {**setup_inputs(rng), **lists(rng, full=True)}
def setup_inputs_hot(rng):
    return {**setup_inputs(rng), **lists(rng, hot=True)}
def setup_inputs_other(rng):
    return {**setup_inputs(rng), **lists(rng, other=True)}
def setup_inputs_repeats(rng):
    return {**setup_inputs(rng), **lists(rng, few=True)}
def setup_inputs_spread(rng):
    d = setup_inputs(rng); d["x"] = wide(rng, N, 128, 4 * T, cols=8); return d
def check_inputs(d):
    b = []
    keys = np.stack([entries(d["ky"][r]) for r in range(N)]).astype(np.int64)
    if keys.min() < 0 or keys.max() > 65535: b.append("ky")
    if len(np.unique(keys & (N * K - 1))) != N * T: b.append("owner and place")
    for r in range(N):
        l = entries(d["lk"][r]).astype(np.int64)
        if np.bincount(keys[r] & (N - 1), minlength=N).max() > CAPP: b.append("CAPP")
        if not np.isin(l, keys).all(): b.append("lk")
        if np.bincount(l & (N - 1), minlength=N).max() > CL: b.append("CL")
    return b
def reference(x, ky, lk, w):
    every = np.concatenate([x[r] for r in range(N)], axis=1)
    number = np.full(65536, -1); number[np.concatenate([entries(ky[r]) for r in range(N)])] = np.arange(N * T)
    y = np.zeros((N, 128, O * S), np.float32)
    for r in range(N):
        v = mx_ref.quantize(cols(every, number[entries(lk[r])]))
        for o in range(O): y[r][:, S * o:S * o + S] = mx_ref.matmul(mx_ref.quantize(np.ascontiguousarray(w[r][:, 512 * o:512 * o + 512])), v)
    return {"y": y}

@@ -1,0 +1,274 @@
+from concourse.bass import DstId, RemoteDMATransfer
+from concourse.mybir import dt, AluOpType as A, ActivationFunctionType as F
+
+C8 = "float8_e4m3fn_x4"
+Z, TC, HC = 16, 512, 256
+DW = 8192
+WIN = Z + 2 * TC
+NX = 2
+XC = TC // NX
+FV = (0, 768, 2048, 2816, 3584, 4736)
+FS = (4736, 5504, 6272, 7040, 7680)
+PRE = ("h", "z3", "z1", "k", "v0", "K", "l", "v1", "L", "z2", "z4", "q0", "s0", "q1", "s1")
+PART = {"0": (0, 16), "1": (16, 32), "f": (0, 32)}
+SEQV = ("gA0", "gB0", "tA", "tB", "sA", "sB", "cA", "cB", "pA", "tC", "pB", "sC", "tD", "cC", "sD", "w-", "cD",
+        "pC", "pD")
+SEQS = ("gA1", "gB1", "gCf", "gDf", "pA", "pB", "pC", "pD")
+SEQT = ("Ca", "Co", "Do", "Da")
+
+SCRATCH = {
+    "kr": ("sbuf", [128, 16], "int32"), "lr": ("sbuf", [128, 32], "int32"),
+    "ka": ("sbuf", [128, 16], "int32"), "la": ("sbuf", [128, 32], "int32"),
+    "ko": ("sbuf", [128, 16], "uint16"), "kp": ("sbuf", [128, 16], "uint16"),
+    "lo": ("sbuf", [128, 64], "uint16"), "rl": ("sbuf", [128, 64], "uint16"),
+    "hr": ("sbuf", [128, 64], "float32"), "hc": ("sbuf", [128, 64], "float32"), "cap": ("sbuf", [128, 64], "float32"),
+    "lw": ("sbuf", [128, 256], "bfloat16"),
+    "vals": ("sbuf", [128, 512], "bfloat16"),
+    "tab": ("sbuf", [128, DW], "bfloat16"),
+    "xb": ("sbuf", [128, 4 * (Z + TC)], "bfloat16"), "wt": ("sbuf", [128, 1024], "bfloat16"),
+    "wq": ("sbuf", [128, 256], C8), "ws": ("sbuf", [128, 256], "uint8"),
+    "pq": ("sbuf", [128, WIN], C8), "ps": ("sbuf", [128, WIN], "uint8"),
+    "sq": ("sbuf", [128, 2 * HC], C8), "ss": ("sbuf", [128, 2 * HC], "uint8"),
+    "oq": ("sbuf", [128, TC], C8), "os8": ("sbuf", [128, TC], "uint8"),
+    "aq": ("sbuf", [128, TC], C8), "as8": ("sbuf", [128, TC], "uint8"),
+    "ysb": ("sbuf", [128, 1024], "float32"),
+    "acc": ("psum", [128, 2048], "float32"),
+}
+for _n in "ABCD":
+    SCRATCH["row" + _n] = ("sbuf", [128, 512], "bfloat16")
+    SCRATCH["tur" + _n] = ("sbuf", [128, 512], "bfloat16")
+    SCRATCH["su" + _n] = ("sbuf", [128, 64], "float32")
+    SCRATCH["of" + _n] = ("sbuf", [128, 16], "uint16")
+
+SEMAPHORES = ["kyl", "lkl", "wl", "hr", "hc", "lw", "cap", "va", "gz", "xz", "dm0", "vz", "sdf", "ka", "la", "sc", "wqs",
+              "ko", "lo", "kar", "rl0", "rl1", "tabs", "p1", "ar0", "ar1", "mm00", "mm01", "mm10", "mm11",
+              "cp00", "cp01", "cp10", "cp11", "st0", "st1", "sent"] + [
+              s + str(h) for s in ("xl", "q") for h in range(NX)] + [
+              s + n for s in ("g", "v", "of", "pc", "ps") for n in "ABCD"]
+
+
+def rank_program(g, core, T, topo):
+    rank = T.rank_of(core)
+    if rank is None:
+        return
+    order = sorted(range(len(T.cores)), key=lambda r: (topo.die(T.cores[r]), r))
+    mine, others = (order[:2], order[2:]) if rank in order[:2] else (order[2:], order[:2])
+    k = mine.index(rank)
+    partner = T.cores[mine[1 - k]]
+    far = [T.cores[r] for r in others]
+    S = T.sem
+    V, SC, SY, TE = g.vector, g.scalar, g.sync, g.tensor
+    cnt = {"sent": 0}
+
+    def engines(dst, part=0, parts=1):
+        e = topo.engines(core, dst)
+        n = len(e) // parts
+        return sum(1 << q for q in e[part * n:part * n + n]), n
+
+    def send(out, in_, sem, dst):
+        m, n = engines(dst)
+        rid, pid, _ = topo.addr(dst)
+        g.remote_dma(out, in_, S[sem], S.sent, pid, rid, m)
+        cnt["sent"] += n
+
+    nsend = len(topo.engines(core, partner))
+    nl = nsend // 2
+    half = {"A": k, "B": 1 - k, "C": k, "D": 1 - k}
+
+    own, par = Z, Z + TC
+    for q, u in ((SY, 0), (SC, 1)):
+        for j in range(2):
+            p = 32 * (2 * j + u)
+            q.dma_start(T.kr[p:p + 32, :], T.ky[:]).then_inc(S.kyl, 16)
+        for j in range(4):
+            p = 16 * (2 * j + u)
+            q.dma_start(T.lr[p:p + 16, :], T.lk[:]).then_inc(S.lkl, 16)
+    for h in range(NX):
+        a = 4 * XC * h
+        SY.dma_start(T.xb[:, 4 * Z + a:4 * Z + a + 4 * XC], T.x[:, a:a + 4 * XC]).then_inc(S["xl%d" % h], 16)
+    SY.wait_ge(S.tabs, 1)
+    SY.dma_start(T.wt[:], T.w[:]).then_inc(S.wl, 16)
+
+    def iota(out, pattern, base, sem):
+        g.iota(out, pattern, base, 0, allow_small_or_imprecise_dtypes=True).then_inc(S[sem], 1)
+
+    iota(T.hr[:], [[TC, 2], [8, 2], [256, 16]], Z + 256 - 8 * 256, "hr")
+    iota(T.lw[:], [[16, 16], [1, 8], [256, 2]], -256, "lw")
+    iota(T.cap[:], [[0, 16], [2048, 4]], 0, "cap")
+    iota(T.tab[:, FS[-1]:DW], [[0, DW - FS[-1]]], 0, "gz")
+    g.wait_ge(S.ko, 1)
+    send(T.kp[:], T.ko[:], "kar", partner)
+    g.wait_ge(S.lo, 2)
+    tr = []
+    for i in range(2):
+        m, n = engines(far[i], i, 2)
+        rid, pid, _ = topo.addr(far[i])
+        tr.append(RemoteDMATransfer(dst_ids=[DstId(rid=rid, pnc=pid)], dma_engine_mask=m, remote_sem=S["rl%d" % k],
+                                    src=T.lo[:, 32 * i:32 * i + 32], dst=T.rl[:, 32 * k:32 * k + 32]))
+        cnt["sent"] += n
+    g.remote_dma_fused(tr, local_sem=S.sent)
+    for h in range(NX):
+        g.wait_ge(S["q%d" % h], 1)
+        a, b = own + XC * h, par + XC * h
+        send(T.pq[:, b:b + XC].bitcast(dt.uint8), T.pq[:, a:a + XC].bitcast(dt.uint8), "p1", partner)
+        send(T.ps[:, b:b + XC], T.ps[:, a:a + XC], "p1", partner)
+    for n in "AB":
+        c, dst = HC * half[n], far[half[n]]
+        g.wait_ge(S["pc" + n], 1)
+        send(T.aq[:, HC * k:HC * k + HC].bitcast(dt.uint8), T.sq[:, c:c + HC].bitcast(dt.uint8), "ar%d" % k, dst)
+        g.wait_ge(S["ps" + n], 1)
+        send(T.as8[:, HC * k:HC * k + HC], T.ss[:, c:c + HC], "ar%d" % k, dst)
+    g.wait_ge(S.sent, cnt["sent"])
+
+    def window(q):
+        for h in range(NX):
+            q.wait_ge(S["q%d" % h], 1)
+        q.wait_ge(S.p1, 2 * NX * nsend)
+
+    def asked(q, n):
+        q.wait_ge(S.tabs, 1)
+        if n in "AB":
+            q.wait_ge(S["rl%d" % half[n]], nl)
+        else:
+            q.wait_ge(S.lo, 2)
+        return (T.rl if n in "AB" else T.lo), 32 * half[n]
+
+    V.memset(T.tab[:, FV[0]:FV[1]], 0.0).then_inc(S.dm0, 1)
+    V.memset(T.xb[:, 0:4 * Z], 0.0).then_inc(S.xz, 1)
+    for op in PRE:
+        what, i = op[0], int(op[1:] or 0)
+        if what == "z":
+            V.memset(T.tab[:, FV[i]:FV[i + 1]], 0.0).then_inc(S.vz, 1)
+        elif what == "h":
+            V.wait_ge(S.hr, 1)
+            V.transpose(T.hc[:], T.hr[:]).then_inc(S.hc, 1)
+        elif what == "v":
+            V.wait_ge(S.lw, 1)
+            V.wait_ge(S.hc, 1)
+            V.tensor_scalar(T.vals[:, HC * i:HC * i + HC], T.lw[:], T.hc[:, 32 * i:32 * i + 1], None,
+                            A.max).then_inc(S.va, 1)
+        elif what == "k":
+            V.wait_ge(S.kyl, 64)
+            V.tensor_scalar(T.ka[:], T.kr[:], DW - 1, None, A.bitwise_and).then_inc(S.ka, 1)
+        elif what == "K":
+            V.wait_ge(S.ka, 1)
+            V.tensor_copy(T.ko[:], T.ka[:]).then_inc(S.ko, 1)
+        elif what == "l":
+            V.wait_ge(S.lkl, 128)
+            V.tensor_scalar(T.la[:], T.lr[:], DW - 1, None, A.bitwise_and).then_inc(S.la, 1)
+        elif what == "L":
+            V.wait_ge(S.la, 1)
+            for d in range(2):
+                V.tensor_copy(T.lo[:, d:64:2], T.la[:]).then_inc(S.lo, 1)
+        elif what == "q":
+            V.wait_ge(S["xl%d" % i], 16)
+            if i == 0:
+                V.wait_ge(S.xz, 1)
+            a, b = (own + XC * i if i else 0), own + XC * i + XC
+            V.quantize_mx(T.pq[:, a:b], T.ps[:, a:b], T.xb[:, 4 * a:4 * b]).then_inc(S["q%d" % i], 1)
+        elif i == 0:
+            V.wait_ge(S.dm0, 1)
+            V.wait_ge(S.vz, len(FV) - 2)
+            V.wait_ge(S.gz, 1)
+            V.wait_ge(S.sdf, len(FS) - 1)
+            V.wait_ge(S.ko, 1)
+            V.wait_ge(S.va, 2)
+            V.tensor_copy(T.tab[:, 0:DW].indirect(T.ko[:, 0:16]), T.vals[:, 0:HC]).then_inc(S.sc, 1)
+        else:
+            V.wait_ge(S.kar, nsend)
+            V.wait_ge(S.sc, 1)
+            V.tensor_copy(T.tab[:, 0:DW].indirect(T.kp[:, 0:16]), T.vals[:, HC:2 * HC]).then_inc(S.tabs, 1)
+
+    first = [1]
+    done = {n: 0 for n in "ABCD"}
+    for op in SEQV:
+        what, n = op[0], op[1]
+        if what == "w":
+            V.wait_ge(S.wl, 16)
+            V.quantize_mx(T.wq[:], T.ws[:], T.wt[:]).then_inc(S.wqs, 1)
+            continue
+        row, tur, su, of = (T[b + n] for b in ("row", "tur", "su", "of"))
+        if what == "g":
+            off, c = asked(V, n)
+            a, b = PART[op[2]]
+            ins = V.tensor_copy(row[:, 16 * a:16 * b], T.tab[:, 0:DW].indirect(off[:, c + a:c + b]))
+        elif what == "p":
+            if first[0]:
+                window(V)
+                first[0] = 0
+            V.wait_ge(S["of" + n], 1)
+            c, out = HC * half[n], (T.sq if n in "AB" else T.oq)
+            V.tensor_copy(out[:, c:c + HC].bitcast(dt.uint32),
+                          T.pq[:, 0:WIN].bitcast(dt.uint32).indirect(of[:, 0:16])).then_inc(S["pc" + n], 1)
+            continue
+        else:
+            if done[n]:
+                V.wait_ge(S["v" + n], done[n])
+            if what == "t":
+                if any(s[:2] == "g" + n for s in SEQS):
+                    V.wait_ge(S["g" + n], 1)
+                ins = V.transpose(tur[:], row[:])
+            elif what == "s":
+                V.wait_ge(S.cap, 1)
+                ins = V.tensor_tensor_scan(su[:], T.cap[:], tur[:, 0:512:8], 0.0, A.min, A.add)
+            else:
+                V.tensor_copy(of[:], su[:, 3:64:4]).then_inc(S["of" + n], 1)
+                continue
+        ins.then_inc(S["v" + n], 1)
+        done[n] += 1
+    for c in (k, 1 - k):
+        V.wait_ge(S["mm0%d" % c], 1)
+        V.tensor_copy(T.ysb[:, HC * c:HC * c + HC],
+                      T.acc[:, 512 * c:512 * c + HC]).then_inc(S["cp0%d" % c], 1)
+
+    SC.wait_ge(S.dm0, 1)
+    for a, b in zip(FS, FS[1:]):
+        SC.activation(T.tab[:, a:b], T.tab[:, 0:b - a], F.Copy).then_inc(S.sdf, 1)
+    first = [1]
+    for op in SEQS:
+        what, n = op[0], op[1]
+        if what == "g":
+            off, c = asked(SC, n)
+            a, b = PART[op[2]]
+            SC.activation(T["row" + n][:, 16 * a:16 * b], T.tab[:, 0:DW].indirect(off[:, c + a:c + b]),
+                          F.Copy).then_inc(S["g" + n], 1)
+        else:
+            if first[0]:
+                window(SC)
+                first[0] = 0
+            SC.wait_ge(S["of" + n], 1)
+            c, out = HC * half[n], (T.ss if n in "AB" else T.os8)
+            SC.activation(out[:, c:c + HC], T.ps[:, 0:WIN].indirect(T["of" + n][:, 0:16]),
+                          F.Copy).then_inc(S["ps" + n], 1)
+    for c in (k, 1 - k):
+        SC.wait_ge(S["mm1%d" % c], 1)
+        a = 512 + HC * c
+        SC.activation(T.ysb[:, a:a + HC], T.acc[:, 1024 + 512 * c:1024 + 512 * c + HC], F.Copy).then_inc(S["cp1%d" % c], 1)
+        SC.wait_ge(S["cp1%d" % c], 1)
+        SC.dma_start(T.y[:, a:a + HC], T.ysb[:, a:a + HC]).then_inc(S.st1, 16)
+    SC.wait_ge(S.st1, 32)
+
+    TE.wait_ge(S.wqs, 1)
+    begun = []
+    for op in SEQT:
+        n, c = op[0], half[op[0]]
+        begin = n not in begun
+        begun.append(n)
+        if op[1] == "o":
+            q, s = T.oq, T.os8
+            TE.wait_ge(S["pc" + n], 1)
+            TE.wait_ge(S["ps" + n], 1)
+        else:
+            q, s = T.aq, T.as8
+            TE.wait_ge(S["ar%d" % c], 2 * nsend)
+        for o in range(2):
+            b = 1024 * o + 512 * c
+            ins = TE.matmul_mx(T.acc[:, b:b + HC], T.wq[:, 128 * o:128 * o + 128], T.ws[:, 128 * o:128 * o + 128],
+                               q[:, HC * c:HC * c + HC], s[:, HC * c:HC * c + HC], begin, not begin)
+            if not begin:
+                ins.then_inc(S["mm%d%d" % (o, c)], 1)
+
+    for c in (k, 1 - k):
+        SY.wait_ge(S["cp0%d" % c], 1)
+        SY.dma_start(T.y[:, HC * c:HC * c + HC], T.ysb[:, HC * c:HC * c + HC]).then_inc(S.st0, 16)
+    SY.wait_ge(S.st0, 32)

@@ -5,22 +5,28 @@ C8 = "float8_e4m3fn_x4"
 Z, TC, HC = 16, 512, 256
 DW = 8192
 WIN = Z + 2 * TC
-NX = 2
-XC = TC // NX
-FV = (0, 768, 2048, 2816, 3584, 4736)
-FS = (4736, 5504, 6272, 7040, 7680)
-PRE = ("h", "z3", "z1", "k", "v0", "K", "l", "v1", "L", "z2", "z4", "q0", "s0", "q1", "s1")
-PART = {"0": (0, 16), "1": (16, 32), "f": (0, 32)}
-SEQV = ("gA0", "gB0", "tA", "tB", "sA", "sB", "cA", "cB", "pA", "tC", "pB", "sC", "tD", "cC", "sD", "w-", "cD",
-        "pC", "pD")
-SEQS = ("gA1", "gB1", "gCf", "gDf", "pA", "pB", "pC", "pD")
-SEQT = ("Ca", "Co", "Do", "Da")
+XC = TC // 2
+CUT = (0, 160, 352, 512)
+CUTR = (0, 160, 352, 512)
+FV = (0, 768, 2048, 2560, 3840)
+FS = (3840, 4608, 5376, 6144, 6400)
+FD = (6400, 7168, 7936)
+PRE = ("z1", "k", "h", "K", "v0", "l", "v1", "T", "z2", "M", "z3", "q0", "s0", "q1", "s1")
+SEQV = ("gR", "gO", "tR", "sR", "tO", "uR", "sO", "pR0", "uO", "pR1", "pO0", "w-", "pR2", "pO1", "pO2", "y00", "y01", "y02")
+SEQS = ("gR", "gO", "pR0", "pR1", "pR2", "pO0", "pO1", "pO2", "y10", "y11", "y12")
+SEQT = ("o0", "a0", "o1", "a1", "o2", "a2")
+SEQG = ("s0", "c0", "s12", "c1", "c2")
+SEQY = ("x0", "z0", "z1", "x1", "w0", "Y00", "Y10", "Y01", "Y11", "Y02", "Y12")
+WW = "tabs"
+KP = 1
+GV = (16, 8)
 
 SCRATCH = {
-    "kr": ("sbuf", [128, 16], "int32"), "lr": ("sbuf", [128, 32], "int32"),
-    "ka": ("sbuf", [128, 16], "int32"), "la": ("sbuf", [128, 32], "int32"),
+    "kr": ("sbuf", [128, 48], "int32"), "ka": ("sbuf", [128, 48], "int32"),
     "ko": ("sbuf", [128, 16], "uint16"), "kp": ("sbuf", [128, 16], "uint16"),
-    "lo": ("sbuf", [128, 64], "uint16"), "rl": ("sbuf", [128, 64], "uint16"),
+    "lf": ("sbuf", [128, 32], "float32"), "lt": ("sbuf", [128, 32], "float32"),
+    "li": ("sbuf", [128, 32], "int32"), "lu": ("sbuf", [128, 32], "uint16"),
+    "lO": ("sbuf", [128, 32], "uint16"), "lR": ("sbuf", [128, 32], "uint16"),
     "hr": ("sbuf", [128, 64], "float32"), "hc": ("sbuf", [128, 64], "float32"), "cap": ("sbuf", [128, 64], "float32"),
     "lw": ("sbuf", [128, 256], "bfloat16"),
     "vals": ("sbuf", [128, 512], "bfloat16"),
@@ -28,23 +34,25 @@ SCRATCH = {
     "xb": ("sbuf", [128, 4 * (Z + TC)], "bfloat16"), "wt": ("sbuf", [128, 1024], "bfloat16"),
     "wq": ("sbuf", [128, 256], C8), "ws": ("sbuf", [128, 256], "uint8"),
     "pq": ("sbuf", [128, WIN], C8), "ps": ("sbuf", [128, WIN], "uint8"),
-    "sq": ("sbuf", [128, 2 * HC], C8), "ss": ("sbuf", [128, 2 * HC], "uint8"),
-    "oq": ("sbuf", [128, TC], C8), "os8": ("sbuf", [128, TC], "uint8"),
+    "qR": ("sbuf", [128, TC], C8), "sR": ("sbuf", [128, TC], "uint8"),
+    "qO": ("sbuf", [128, TC], C8), "sO": ("sbuf", [128, TC], "uint8"),
     "aq": ("sbuf", [128, TC], C8), "as8": ("sbuf", [128, TC], "uint8"),
     "ysb": ("sbuf", [128, 1024], "float32"),
-    "acc": ("psum", [128, 2048], "float32"),
+    "acc": ("psum", [128, 4096], "float32"),
 }
-for _n in "ABCD":
+for _n in "RO":
     SCRATCH["row" + _n] = ("sbuf", [128, 512], "bfloat16")
     SCRATCH["tur" + _n] = ("sbuf", [128, 512], "bfloat16")
-    SCRATCH["su" + _n] = ("sbuf", [128, 64], "float32")
-    SCRATCH["of" + _n] = ("sbuf", [128, 16], "uint16")
+    SCRATCH["su" + _n] = ("sbuf", [128, 128], "float32" if "c" + _n in SEQV else "uint16")
+    SCRATCH["st" + _n] = ("sbuf", [128, 32], "float32")
+    SCRATCH["of" + _n] = ("sbuf", [128, 32], "uint16")
 
-SEMAPHORES = ["kyl", "lkl", "wl", "hr", "hc", "lw", "cap", "va", "gz", "xz", "dm0", "vz", "sdf", "ka", "la", "sc", "wqs",
-              "ko", "lo", "kar", "rl0", "rl1", "tabs", "p1", "ar0", "ar1", "mm00", "mm01", "mm10", "mm11",
-              "cp00", "cp01", "cp10", "cp11", "st0", "st1", "sent"] + [
-              s + str(h) for s in ("xl", "q") for h in range(NX)] + [
-              s + n for s in ("g", "v", "of", "pc", "ps") for n in "ABCD"]
+NP = len(CUT) - 1
+SEMAPHORES = ["kyl", "lkl", "wl", "hr", "hc", "lw", "cap", "va", "gz", "xz", "dm0", "vz", "sz", "dz", "ka", "la", "lf",
+              "lt", "sc", "wqs", "ko", "lo", "kar", "rl", "tabs", "p1", "st0", "st1", "sent", "xl0", "xl1", "q0", "q1"] + [
+              s + n for s in ("g", "v", "of") for n in "RO"] + [
+              s + str(j) for s in ("pcO", "psO", "mm0", "mm1", "cp0", "cp1") for j in range(NP)] + [
+              s + str(j) for s in ("pcR", "psR") for j in range(len(CUTR) - 1)] + ["ar" + op for op in SEQG]
 
 
 def rank_program(g, core, T, topo):
@@ -52,42 +60,52 @@ def rank_program(g, core, T, topo):
     if rank is None:
         return
     order = sorted(range(len(T.cores)), key=lambda r: (topo.die(T.cores[r]), r))
-    mine, others = (order[:2], order[2:]) if rank in order[:2] else (order[2:], order[:2])
-    k = mine.index(rank)
-    partner = T.cores[mine[1 - k]]
-    far = [T.cores[r] for r in others]
+    k = order.index(rank)
+    partner, mate = T.cores[order[(k + 2) % 4]], T.cores[order[k - k % 2 + 1 - k % 2]]
     S = T.sem
     V, SC, SY, TE = g.vector, g.scalar, g.sync, g.tensor
-    cnt = {"sent": 0}
+    sent = [0]
 
-    def engines(dst, part=0, parts=1):
+    def send(out, in_, sem, dst, part=0, parts=1):
+        rid, pid, _ = topo.addr(dst)
         e = topo.engines(core, dst)
         n = len(e) // parts
-        return sum(1 << q for q in e[part * n:part * n + n]), n
+        g.remote_dma(out, in_, S[sem], S.sent, pid, rid, sum(1 << q for q in e[part * n:part * n + n]))
+        sent[0] += n
 
-    def send(out, in_, sem, dst):
-        m, n = engines(dst)
-        rid, pid, _ = topo.addr(dst)
-        g.remote_dma(out, in_, S[sem], S.sent, pid, rid, m)
-        cnt["sent"] += n
+    def store(q, op, sem):
+        o, j = int(op[1]), int(op[2])
+        a, b = TC * o + CUT[j], TC * o + CUT[j + 1]
+        q.wait_ge(S["cp" + op[1:]], 1)
+        q.dma_start(T.y[:, a:b], T.ysb[:, a:b]).then_inc(sem, 16)
 
-    nsend = len(topo.engines(core, partner))
-    nl = nsend // 2
-    half = {"A": k, "B": 1 - k, "C": k, "D": 1 - k}
+    def result(op):
+        o, j = int(op[1]), int(op[2])
+        a, n = 1024 * j + 512 * o, CUT[j + 1] - CUT[j]
+        return T.ysb[:, TC * o + CUT[j]:TC * o + CUT[j + 1]], T.acc[:, a:a + n]
+
+    par_n, mate_n = len(topo.engines(partner, core)), len(topo.engines(mate, core))
 
     own, par = Z, Z + TC
-    for q, u in ((SY, 0), (SC, 1)):
-        for j in range(2):
-            p = 32 * (2 * j + u)
-            q.dma_start(T.kr[p:p + 32, :], T.ky[:]).then_inc(S.kyl, 16)
-        for j in range(4):
-            p = 16 * (2 * j + u)
-            q.dma_start(T.lr[p:p + 16, :], T.lk[:]).then_inc(S.lkl, 16)
-    for h in range(NX):
-        a = 4 * XC * h
-        SY.dma_start(T.xb[:, 4 * Z + a:4 * Z + a + 4 * XC], T.x[:, a:a + 4 * XC]).then_inc(S["xl%d" % h], 16)
-    SY.wait_ge(S.tabs, 1)
-    SY.dma_start(T.wt[:], T.w[:]).then_inc(S.wl, 16)
+    for c, src, sem in ((0, T.ky, S.kyl), (16, T.lk, S.lkl), (32, T.lk, S.lkl)):
+        for q, u in ((SY, 0), (SC, 1)):
+            for j in range(2):
+                p = 32 * (2 * j + u)
+                q.dma_start(T.kr[p:p + 32, c:c + 16], src[:]).then_inc(sem, 16)
+    for op in SEQY:
+        what, i = op[0], int(op[1])
+        if what == "x":
+            a = 4 * XC * i
+            SY.dma_start(T.xb[:, 4 * Z + a:4 * Z + a + 4 * XC], T.x[:, a:a + 4 * XC]).then_inc(S["xl%d" % i], 16)
+        elif what == "z":
+            SY.wait_ge(S.dm0, 1)
+            SY.dma_start(T.tab[:, FD[i]:FD[i + 1]], T.tab[:, 0:FD[i + 1] - FD[i]]).then_inc(S.dz, 16)
+        elif what == "w":
+            SY.wait_ge(S[WW], 1)
+            SY.dma_start(T.wt[:], T.w[:]).then_inc(S.wl, 16)
+        else:
+            store(SY, op, S.st0)
+    SY.wait_ge(S.st0, 16 * sum(op[0] == "Y" for op in SEQY))
 
     def iota(out, pattern, base, sem):
         g.iota(out, pattern, base, 0, allow_small_or_imprecise_dtypes=True).then_inc(S[sem], 1)
@@ -95,43 +113,45 @@ def rank_program(g, core, T, topo):
     iota(T.hr[:], [[TC, 2], [8, 2], [256, 16]], Z + 256 - 8 * 256, "hr")
     iota(T.lw[:], [[16, 16], [1, 8], [256, 2]], -256, "lw")
     iota(T.cap[:], [[0, 16], [2048, 4]], 0, "cap")
-    iota(T.tab[:, FS[-1]:DW], [[0, DW - FS[-1]]], 0, "gz")
+    if FD[-1] < DW:
+        iota(T.tab[:, FD[-1]:DW], [[0, DW - FD[-1]]], 0, "gz")
     g.wait_ge(S.ko, 1)
-    send(T.kp[:], T.ko[:], "kar", partner)
-    g.wait_ge(S.lo, 2)
-    tr = []
-    for i in range(2):
-        m, n = engines(far[i], i, 2)
-        rid, pid, _ = topo.addr(far[i])
-        tr.append(RemoteDMATransfer(dst_ids=[DstId(rid=rid, pnc=pid)], dma_engine_mask=m, remote_sem=S["rl%d" % k],
-                                    src=T.lo[:, 32 * i:32 * i + 32], dst=T.rl[:, 32 * k:32 * k + 32]))
-        cnt["sent"] += n
-    g.remote_dma_fused(tr, local_sem=S.sent)
-    for h in range(NX):
+    send(T.kp[:], T.ko[:], "kar", partner, 0, KP)
+    g.wait_ge(S.lo, 1)
+    send(T.lR[:], T.lO[:], "rl", mate, KP - 1, KP)
+    for h in range(2):
         g.wait_ge(S["q%d" % h], 1)
         a, b = own + XC * h, par + XC * h
         send(T.pq[:, b:b + XC].bitcast(dt.uint8), T.pq[:, a:a + XC].bitcast(dt.uint8), "p1", partner)
-        send(T.ps[:, b:b + XC], T.ps[:, a:a + XC], "p1", partner)
-    for n in "AB":
-        c, dst = HC * half[n], far[half[n]]
-        g.wait_ge(S["pc" + n], 1)
-        send(T.aq[:, HC * k:HC * k + HC].bitcast(dt.uint8), T.sq[:, c:c + HC].bitcast(dt.uint8), "ar%d" % k, dst)
-        g.wait_ge(S["ps" + n], 1)
-        send(T.as8[:, HC * k:HC * k + HC], T.ss[:, c:c + HC], "ar%d" % k, dst)
-    g.wait_ge(S.sent, cnt["sent"])
+    send(T.ps[:, par:par + TC], T.ps[:, own:own + TC], "p1", partner)
+    for op in SEQG:
+        a, b = CUTR[int(op[1])], CUTR[int(op[-1]) + 1]
+        for j in op[1:]:
+            g.wait_ge(S["p%sR%s" % (op[0], j)], 1)
+        if op[0] == "c":
+            send(T.aq[:, a:b].bitcast(dt.uint8), T.qR[:, a:b].bitcast(dt.uint8), "ar" + op, mate)
+        else:
+            send(T.as8[:, a:b], T.sR[:, a:b], "ar" + op, mate)
+    g.wait_ge(S.sent, sent[0])
 
     def window(q):
-        for h in range(NX):
-            q.wait_ge(S["q%d" % h], 1)
-        q.wait_ge(S.p1, 2 * NX * nsend)
+        q.wait_ge(S.q0, 1)
+        q.wait_ge(S.q1, 1)
+        q.wait_ge(S.p1, 3 * par_n)
 
     def asked(q, n):
         q.wait_ge(S.tabs, 1)
-        if n in "AB":
-            q.wait_ge(S["rl%d" % half[n]], nl)
+        if n == "R":
+            q.wait_ge(S.rl, mate_n // KP)
         else:
-            q.wait_ge(S.lo, 2)
-        return (T.rl if n in "AB" else T.lo), 32 * half[n]
+            q.wait_ge(S.lo, 1)
+
+    def quantise(i):
+        V.wait_ge(S["xl%d" % i], 16)
+        if i == 0:
+            V.wait_ge(S.xz, 1)
+        a, b = (own + XC if i else 0), own + XC * i + XC
+        V.quantize_mx(T.pq[:, a:b], T.ps[:, a:b], T.xb[:, 4 * a:4 * b]).then_inc(S["q%d" % i], 1)
 
     V.memset(T.tab[:, FV[0]:FV[1]], 0.0).then_inc(S.dm0, 1)
     V.memset(T.xb[:, 0:4 * Z], 0.0).then_inc(S.xz, 1)
@@ -149,126 +169,155 @@ def rank_program(g, core, T, topo):
                             A.max).then_inc(S.va, 1)
         elif what == "k":
             V.wait_ge(S.kyl, 64)
+            V.tensor_scalar(T.ka[:, 0:16], T.kr[:, 0:16], DW - 1, None, A.bitwise_and).then_inc(S.ka, 1)
+        elif what == "l":
+            V.wait_ge(S.lkl, 128)
+            V.tensor_scalar(T.ka[:, 16:48], T.kr[:, 16:48], DW - 1, None, A.bitwise_and).then_inc(S.la, 1)
+        elif what == "b":
+            V.wait_ge(S.kyl, 64)
+            V.wait_ge(S.lkl, 128)
             V.tensor_scalar(T.ka[:], T.kr[:], DW - 1, None, A.bitwise_and).then_inc(S.ka, 1)
         elif what == "K":
             V.wait_ge(S.ka, 1)
-            V.tensor_copy(T.ko[:], T.ka[:]).then_inc(S.ko, 1)
-        elif what == "l":
-            V.wait_ge(S.lkl, 128)
-            V.tensor_scalar(T.la[:], T.lr[:], DW - 1, None, A.bitwise_and).then_inc(S.la, 1)
-        elif what == "L":
+            V.tensor_copy(T.ko[:], T.ka[:, 0:16]).then_inc(S.ko, 1)
+        elif what == "d":
+            V.wait_ge(S.ka if "b" in PRE else S.la, 1)
+            V.tensor_copy(T.lf[:], T.ka[:, 16:48]).then_inc(S.lf, 1)
+        elif what == "t":
+            V.wait_ge(S.lf, 1)
+            V.transpose(T.lt[:], T.lf[:]).then_inc(S.lt, 1)
+        elif what == "T":
+            V.wait_ge(S.ka if "b" in PRE else S.la, 1)
+            V.transpose(T.li[:], T.ka[:, 16:48]).then_inc(S.lt, 1)
+        elif what == "D":
             V.wait_ge(S.la, 1)
-            for d in range(2):
-                V.tensor_copy(T.lo[:, d:64:2], T.la[:]).then_inc(S.lo, 1)
+            V.tensor_copy(T.lu[:], T.ka[:, 16:48]).then_inc(S.lf, 1)
+        elif what == "U":
+            V.wait_ge(S.lf, 1)
+            V.transpose(T.lO[:], T.lu[:]).then_inc(S.lo, 1)
+        elif what == "M":
+            V.wait_ge(S.lt, 1)
+            V.tensor_copy(T.lO[:], T.li[:]).then_inc(S.lo, 1)
+        elif what == "L":
+            V.wait_ge(S.lt, 1)
+            V.tensor_copy(T.lO[:], T.lt[:]).then_inc(S.lo, 1)
         elif what == "q":
-            V.wait_ge(S["xl%d" % i], 16)
-            if i == 0:
-                V.wait_ge(S.xz, 1)
-            a, b = (own + XC * i if i else 0), own + XC * i + XC
-            V.quantize_mx(T.pq[:, a:b], T.ps[:, a:b], T.xb[:, 4 * a:4 * b]).then_inc(S["q%d" % i], 1)
+            quantise(i)
+        elif what == "w":
+            V.wait_ge(S.wl, 16)
+            V.quantize_mx(T.wq[:], T.ws[:], T.wt[:]).then_inc(S.wqs, 1)
         elif i == 0:
             V.wait_ge(S.dm0, 1)
             V.wait_ge(S.vz, len(FV) - 2)
-            V.wait_ge(S.gz, 1)
-            V.wait_ge(S.sdf, len(FS) - 1)
+            if FD[-1] < DW:
+                V.wait_ge(S.gz, 1)
+            V.wait_ge(S.sz, len(FS) - 1)
+            if len(FD) > 1:
+                V.wait_ge(S.dz, 16 * (len(FD) - 1))
             V.wait_ge(S.ko, 1)
             V.wait_ge(S.va, 2)
             V.tensor_copy(T.tab[:, 0:DW].indirect(T.ko[:, 0:16]), T.vals[:, 0:HC]).then_inc(S.sc, 1)
         else:
-            V.wait_ge(S.kar, nsend)
+            V.wait_ge(S.kar, par_n // KP)
             V.wait_ge(S.sc, 1)
             V.tensor_copy(T.tab[:, 0:DW].indirect(T.kp[:, 0:16]), T.vals[:, HC:2 * HC]).then_inc(S.tabs, 1)
 
     first = [1]
-    done = {n: 0 for n in "ABCD"}
+    done = {"R": 0, "O": 0}
     for op in SEQV:
         what, n = op[0], op[1]
         if what == "w":
             V.wait_ge(S.wl, 16)
             V.quantize_mx(T.wq[:], T.ws[:], T.wt[:]).then_inc(S.wqs, 1)
             continue
-        row, tur, su, of = (T[b + n] for b in ("row", "tur", "su", "of"))
-        if what == "g":
-            off, c = asked(V, n)
-            a, b = PART[op[2]]
-            ins = V.tensor_copy(row[:, 16 * a:16 * b], T.tab[:, 0:DW].indirect(off[:, c + a:c + b]))
-        elif what == "p":
+        if what == "q":
+            quantise(int(n))
+            continue
+        if what == "y":
+            V.wait_ge(S["mm" + op[1:]], 1)
+            V.tensor_copy(*result(op)).then_inc(S["cp" + op[1:]], 1)
+            continue
+        row, tur, su, st, of = (T[b + n] for b in ("row", "tur", "su", "st", "of"))
+        if what == "p":
             if first[0]:
                 window(V)
                 first[0] = 0
             V.wait_ge(S["of" + n], 1)
-            c, out = HC * half[n], (T.sq if n in "AB" else T.oq)
-            V.tensor_copy(out[:, c:c + HC].bitcast(dt.uint32),
-                          T.pq[:, 0:WIN].bitcast(dt.uint32).indirect(of[:, 0:16])).then_inc(S["pc" + n], 1)
+            a, b = (CUTR if n == "R" else CUT)[int(op[2]):int(op[2]) + 2]
+            V.tensor_copy(T["q" + n][:, a:b].bitcast(dt.uint32),
+                          T.pq[:, 0:WIN].bitcast(dt.uint32).indirect(of[:, a // 16:b // 16])).then_inc(S["pc" + op[1:]], 1)
+            continue
+        if done[n]:
+            V.wait_ge(S["v" + n], done[n])
+        if what == "g":
+            asked(V, n)
+            c = GV["RO".index(n)]
+            calls = [V.tensor_copy(row[:, 0:16 * c], T.tab[:, 0:DW].indirect(T["l" + n][:, 0:c]))]
+        elif what == "t":
+            V.wait_ge(S["g" + n], 1)
+            calls = [V.transpose(tur[:], row[:])]
+        elif what == "s":
+            V.wait_ge(S.cap, 1)
+            calls = [V.tensor_tensor_scan(su[:, 64 * d:64 * d + 64], T.cap[:], tur[:, 0:512:8], 0.0, A.min, A.add)
+                     for d in range(2)]
+        elif what == "u" and "c" + n in SEQV:
+            calls = [V.transpose(st[:], su[:, 3:128:4])]
+        elif what == "u":
+            V.transpose(of[:], su[:, 3:128:4]).then_inc(S["of" + n], 1)
             continue
         else:
-            if done[n]:
-                V.wait_ge(S["v" + n], done[n])
-            if what == "t":
-                if any(s[:2] == "g" + n for s in SEQS):
-                    V.wait_ge(S["g" + n], 1)
-                ins = V.transpose(tur[:], row[:])
-            elif what == "s":
-                V.wait_ge(S.cap, 1)
-                ins = V.tensor_tensor_scan(su[:], T.cap[:], tur[:, 0:512:8], 0.0, A.min, A.add)
-            else:
-                V.tensor_copy(of[:], su[:, 3:64:4]).then_inc(S["of" + n], 1)
-                continue
-        ins.then_inc(S["v" + n], 1)
-        done[n] += 1
-    for c in (k, 1 - k):
-        V.wait_ge(S["mm0%d" % c], 1)
-        V.tensor_copy(T.ysb[:, HC * c:HC * c + HC],
-                      T.acc[:, 512 * c:512 * c + HC]).then_inc(S["cp0%d" % c], 1)
+            V.tensor_copy(of[:], st[:]).then_inc(S["of" + n], 1)
+            continue
+        for ins in calls:
+            ins.then_inc(S["v" + n], 1)
+        done[n] += len(calls)
 
     SC.wait_ge(S.dm0, 1)
     for a, b in zip(FS, FS[1:]):
-        SC.activation(T.tab[:, a:b], T.tab[:, 0:b - a], F.Copy).then_inc(S.sdf, 1)
+        SC.activation(T.tab[:, a:b], T.tab[:, 0:b - a], F.Copy).then_inc(S.sz, 1)
     first = [1]
     for op in SEQS:
         what, n = op[0], op[1]
         if what == "g":
-            off, c = asked(SC, n)
-            a, b = PART[op[2]]
-            SC.activation(T["row" + n][:, 16 * a:16 * b], T.tab[:, 0:DW].indirect(off[:, c + a:c + b]),
+            asked(SC, n)
+            a = GV["RO".index(n)] if "g" + n in SEQV else 0
+            SC.activation(T["row" + n][:, 16 * a:512], T.tab[:, 0:DW].indirect(T["l" + n][:, a:32]),
                           F.Copy).then_inc(S["g" + n], 1)
+        elif what == "y":
+            SC.wait_ge(S["mm" + op[1:]], 1)
+            SC.activation(*result(op), F.Copy).then_inc(S["cp" + op[1:]], 1)
+        elif what == "Y":
+            store(SC, op, S.st1)
         else:
             if first[0]:
                 window(SC)
                 first[0] = 0
             SC.wait_ge(S["of" + n], 1)
-            c, out = HC * half[n], (T.ss if n in "AB" else T.os8)
-            SC.activation(out[:, c:c + HC], T.ps[:, 0:WIN].indirect(T["of" + n][:, 0:16]),
-                          F.Copy).then_inc(S["ps" + n], 1)
-    for c in (k, 1 - k):
-        SC.wait_ge(S["mm1%d" % c], 1)
-        a = 512 + HC * c
-        SC.activation(T.ysb[:, a:a + HC], T.acc[:, 1024 + 512 * c:1024 + 512 * c + HC], F.Copy).then_inc(S["cp1%d" % c], 1)
-        SC.wait_ge(S["cp1%d" % c], 1)
-        SC.dma_start(T.y[:, a:a + HC], T.ysb[:, a:a + HC]).then_inc(S.st1, 16)
-    SC.wait_ge(S.st1, 32)
+            a, b = (CUTR if n == "R" else CUT)[int(op[2]):int(op[2]) + 2]
+            SC.activation(T["s" + n][:, a:b], T.ps[:, 0:WIN].indirect(T["of" + n][:, a // 16:b // 16]),
+                          F.Copy).then_inc(S["ps" + op[1:]], 1)
+    if any(op[0] == "Y" for op in SEQS):
+        SC.wait_ge(S.st1, 16 * sum(op[0] == "Y" for op in SEQS))
 
     TE.wait_ge(S.wqs, 1)
     begun = []
     for op in SEQT:
-        n, c = op[0], half[op[0]]
-        begin = n not in begun
-        begun.append(n)
-        if op[1] == "o":
-            q, s = T.oq, T.os8
-            TE.wait_ge(S["pc" + n], 1)
-            TE.wait_ge(S["ps" + n], 1)
+        j = int(op[1])
+        a, b = CUT[j], CUT[j + 1]
+        begin = j not in begun
+        begun.append(j)
+        if op[0] == "o":
+            q, s = T.qO, T.sO
+            TE.wait_ge(S["pcO%d" % j], 1)
+            TE.wait_ge(S["psO%d" % j], 1)
         else:
             q, s = T.aq, T.as8
-            TE.wait_ge(S["ar%d" % c], 2 * nsend)
+            for sent_op in SEQG:
+                if CUTR[int(sent_op[1])] < b and a < CUTR[int(sent_op[-1]) + 1]:
+                    TE.wait_ge(S["ar" + sent_op], mate_n)
         for o in range(2):
-            b = 1024 * o + 512 * c
-            ins = TE.matmul_mx(T.acc[:, b:b + HC], T.wq[:, 128 * o:128 * o + 128], T.ws[:, 128 * o:128 * o + 128],
-                               q[:, HC * c:HC * c + HC], s[:, HC * c:HC * c + HC], begin, not begin)
+            c = 1024 * j + 512 * o
+            ins = TE.matmul_mx(T.acc[:, c:c + b - a], T.wq[:, 128 * o:128 * o + 128], T.ws[:, 128 * o:128 * o + 128],
+                               q[:, a:b], s[:, a:b], begin, not begin)
             if not begin:
-                ins.then_inc(S["mm%d%d" % (o, c)], 1)
-
-    for c in (k, 1 - k):
-        SY.wait_ge(S["cp0%d" % c], 1)
-        SY.dma_start(T.y[:, HC * c:HC * c + HC], T.ysb[:, HC * c:HC * c + HC]).then_inc(S.st0, 16)
-    SY.wait_ge(S.st0, 32)
+                ins.then_inc(S["mm%d%d" % (o, j)], 1)

@@ -5,29 +5,32 @@ C8 = "float8_e4m3fn_x4"
 Z, TC, HC = 16, 512, 256
 DW = 8192
 WIN = Z + 2 * TC
-XC = TC // 2
+XCUT = (0, 256, 512)
+SEQX = ("c0", "c1", "s01")
 CUT = (0, 160, 352, 512)
 CUTR = (0, 160, 352, 512)
-FV = (0, 768, 2048, 2560, 3840)
-FS = (3840, 4608, 5376, 6144, 6400)
-FD = (6400, 7168, 7936)
-PRE = ("z1", "k", "h", "K", "v0", "l", "v1", "T", "z2", "M", "z3", "q0", "s0", "q1", "s1")
-SEQV = ("gR", "gO", "tR", "sR", "tO", "uR", "sO", "pR0", "uO", "pR1", "pO0", "w-", "pR2", "pO1", "pO2", "y00", "y01", "y02")
-SEQS = ("gR", "gO", "pR0", "pR1", "pR2", "pO0", "pO1", "pO2", "y10", "y11", "y12")
+FV = (0, 640, 1792, 1920, 2944, 3968)
+FS = (3968, 4608, 6272)
+FD = (6272, 6912, 7936)
+PRE = ("z1", "h", "z2", "k", "x", "v0", "K", "z3", "l", "z4", "D0", "D1", "q0", "U", "s0", "q1", "s1")
+SEQV = ("gR", "gO", "tR", "aO", "sR", "bO", "uR", "sO", "pR0", "uO", "pR1", "w-", "pO0", "pR2", "pO1", "pO2", "y00", "y01", "y02")
+SEQS = ("gR", "gOa", "gOb", "pR0", "pR1", "pR2", "pO0", "pO1", "pO2", "y10", "y11", "y12")
 SEQT = ("o0", "a0", "o1", "a1", "o2", "a2")
-SEQG = ("s0", "c0", "s12", "c1", "c2")
-SEQY = ("x0", "z0", "z1", "x1", "w0", "Y00", "Y10", "Y01", "Y11", "Y02", "Y12")
+SEQG = ("c0", "s0", "c1", "s12", "c2")
+SEQY = ("x0", "l0", "l1", "z0", "z1", "x1", "w0", "Y00", "Y10", "Y01", "Y11", "Y02", "Y12")
 WW = "tabs"
-KP = 1
+CAPL = 1
+NL = 1
+KP = 2
 GV = (16, 8)
 
 SCRATCH = {
     "kr": ("sbuf", [128, 48], "int32"), "ka": ("sbuf", [128, 48], "int32"),
-    "ko": ("sbuf", [128, 16], "uint16"), "kp": ("sbuf", [128, 16], "uint16"),
+    "ko": ("sbuf", [128, 48], "uint16"), "kp": ("sbuf", [128, 16], "uint16"),
     "lf": ("sbuf", [128, 32], "float32"), "lt": ("sbuf", [128, 32], "float32"),
     "li": ("sbuf", [128, 32], "int32"), "lu": ("sbuf", [128, 32], "uint16"),
     "lO": ("sbuf", [128, 32], "uint16"), "lR": ("sbuf", [128, 32], "uint16"),
-    "hr": ("sbuf", [128, 64], "float32"), "hc": ("sbuf", [128, 64], "float32"), "cap": ("sbuf", [128, 64], "float32"),
+    "hr": ("sbuf", [128, 64], "bfloat16"), "hc": ("sbuf", [128, 64], "bfloat16"), "cap": ("sbuf", [128, 64], "float32"),
     "lw": ("sbuf", [128, 256], "bfloat16"),
     "vals": ("sbuf", [128, 512], "bfloat16"),
     "tab": ("sbuf", [128, DW], "bfloat16"),
@@ -48,8 +51,8 @@ for _n in "RO":
     SCRATCH["of" + _n] = ("sbuf", [128, 32], "uint16")
 
 NP = len(CUT) - 1
-SEMAPHORES = ["kyl", "lkl", "wl", "hr", "hc", "lw", "cap", "va", "gz", "xz", "dm0", "vz", "sz", "dz", "ka", "la", "lf",
-              "lt", "sc", "wqs", "ko", "lo", "kar", "rl", "tabs", "p1", "st0", "st1", "sent", "xl0", "xl1", "q0", "q1"] + [
+SEMAPHORES = ["dup", "dm1", "gOa", "gOb", "kyl", "lkl", "wl", "hr", "hc", "lw", "cap", "va0", "va1", "gz", "xz", "dm0", "vz", "sz", "dz", "ka", "la", "lf",
+              "lt", "sc", "wqs", "ko", "lo", "kar", "rl", "tabs", "p1", "st0", "st1", "sent", "xl0", "xl1", "xl2", "q0", "q1", "q2"] + [
               s + n for s in ("g", "v", "of") for n in "RO"] + [
               s + str(j) for s in ("pcO", "psO", "mm0", "mm1", "cp0", "cp1") for j in range(NP)] + [
               s + str(j) for s in ("pcR", "psR") for j in range(len(CUTR) - 1)] + ["ar" + op for op in SEQG]
@@ -87,19 +90,29 @@ def rank_program(g, core, T, topo):
     par_n, mate_n = len(topo.engines(partner, core)), len(topo.engines(mate, core))
 
     own, par = Z, Z + TC
-    for c, src, sem in ((0, T.ky, S.kyl), (16, T.lk, S.lkl), (32, T.lk, S.lkl)):
+    for c, src, sem in ((0, T.ky, S.kyl), (16, T.lk, S.lkl), (32, T.lk, S.lkl))[:1 + NL]:
         for q, u in ((SY, 0), (SC, 1)):
             for j in range(2):
                 p = 32 * (2 * j + u)
-                q.dma_start(T.kr[p:p + 32, c:c + 16], src[:]).then_inc(sem, 16)
+                if c == 0 or (u and c == 16) or "l0" not in SEQY:
+                    q.dma_start(T.kr[p:p + 32, c:c + 16], src[:]).then_inc(sem, 16)
     for op in SEQY:
         what, i = op[0], int(op[1])
-        if what == "x":
-            a = 4 * XC * i
-            SY.dma_start(T.xb[:, 4 * Z + a:4 * Z + a + 4 * XC], T.x[:, a:a + 4 * XC]).then_inc(S["xl%d" % i], 16)
+        if what == "l":
+            SY.dma_start(T.kr[64 * i:64 * i + 32, 16:32], T.lk[:]).then_inc(S.lkl, 16)
+        elif what == "m":
+            SY.dma_start(T.kr[32 * i:32 * i + 32, 32:48], T.lk[:]).then_inc(S.lkl, 16)
+        elif what == "x":
+            a, b = 4 * XCUT[i], 4 * XCUT[i + 1]
+            SY.dma_start(T.xb[:, 4 * Z + a:4 * Z + b], T.x[:, a:b]).then_inc(S["xl%d" % i], 16)
         elif what == "z":
             SY.wait_ge(S.dm0, 1)
+            if FD[i + 1] - FD[i] > FV[1]:
+                SY.wait_ge(S.dm1, 1)
             SY.dma_start(T.tab[:, FD[i]:FD[i + 1]], T.tab[:, 0:FD[i + 1] - FD[i]]).then_inc(S.dz, 16)
+        elif what == "d":
+            SY.wait_ge(S.lkl, 64)
+            SY.dma_start(T.kr[:, 32:48], T.kr[:, 16:32]).then_inc(S.dup, 16)
         elif what == "w":
             SY.wait_ge(S[WW], 1)
             SY.dma_start(T.wt[:], T.w[:]).then_inc(S.wl, 16)
@@ -110,20 +123,30 @@ def rank_program(g, core, T, topo):
     def iota(out, pattern, base, sem):
         g.iota(out, pattern, base, 0, allow_small_or_imprecise_dtypes=True).then_inc(S[sem], 1)
 
-    iota(T.hr[:], [[TC, 2], [8, 2], [256, 16]], Z + 256 - 8 * 256, "hr")
+    if "v1" in PRE:
+        iota(T.hr[:], [[TC, 2], [8, 2], [256, 16]], Z + 256 - 8 * 256, "hr")
+    else:
+        iota(T.hr[:, 0:32], [[8, 2], [256, 16]], Z + 256 - 8 * 256, "hr")
+        iota(T.hr[:, 32:64], [[0, 2], [TC // 8, 16]], 0, "hr")
     iota(T.lw[:], [[16, 16], [1, 8], [256, 2]], -256, "lw")
-    iota(T.cap[:], [[0, 16], [2048, 4]], 0, "cap")
+    if not CAPL:
+        iota(T.cap[:], [[0, 16], [2048, 4]], 0, "cap")
     if FD[-1] < DW:
         iota(T.tab[:, FD[-1]:DW], [[0, DW - FD[-1]]], 0, "gz")
     g.wait_ge(S.ko, 1)
-    send(T.kp[:], T.ko[:], "kar", partner, 0, KP)
+    send(T.kp[:], T.ko[:, 0:16], "kar", partner, 0, KP)
     g.wait_ge(S.lo, 1)
     send(T.lR[:], T.lO[:], "rl", mate, KP - 1, KP)
-    for h in range(2):
-        g.wait_ge(S["q%d" % h], 1)
-        a, b = own + XC * h, par + XC * h
-        send(T.pq[:, b:b + XC].bitcast(dt.uint8), T.pq[:, a:a + XC].bitcast(dt.uint8), "p1", partner)
-    send(T.ps[:, par:par + TC], T.ps[:, own:own + TC], "p1", partner)
+    if CAPL:
+        iota(T.cap[:], [[0, 16], [2048, 4]], 0, "cap")
+    for op in SEQX:
+        a, b = XCUT[int(op[1])], XCUT[int(op[-1]) + 1]
+        for h in op[1:]:
+            g.wait_ge(S["q" + h], 1)
+        if op[0] == "c":
+            send(T.pq[:, par + a:par + b].bitcast(dt.uint8), T.pq[:, own + a:own + b].bitcast(dt.uint8), "p1", partner)
+        else:
+            send(T.ps[:, par + a:par + b], T.ps[:, own + a:own + b], "p1", partner)
     for op in SEQG:
         a, b = CUTR[int(op[1])], CUTR[int(op[-1]) + 1]
         for j in op[1:]:
@@ -135,9 +158,9 @@ def rank_program(g, core, T, topo):
     g.wait_ge(S.sent, sent[0])
 
     def window(q):
-        q.wait_ge(S.q0, 1)
-        q.wait_ge(S.q1, 1)
-        q.wait_ge(S.p1, 3 * par_n)
+        for h in range(len(XCUT) - 1):
+            q.wait_ge(S["q%d" % h], 1)
+        q.wait_ge(S.p1, len(SEQX) * par_n)
 
     def asked(q, n):
         q.wait_ge(S.tabs, 1)
@@ -150,36 +173,46 @@ def rank_program(g, core, T, topo):
         V.wait_ge(S["xl%d" % i], 16)
         if i == 0:
             V.wait_ge(S.xz, 1)
-        a, b = (own + XC if i else 0), own + XC * i + XC
+        a, b = (own + XCUT[i] if i else 0), own + XCUT[i + 1]
         V.quantize_mx(T.pq[:, a:b], T.ps[:, a:b], T.xb[:, 4 * a:4 * b]).then_inc(S["q%d" % i], 1)
 
     V.memset(T.tab[:, FV[0]:FV[1]], 0.0).then_inc(S.dm0, 1)
-    V.memset(T.xb[:, 0:4 * Z], 0.0).then_inc(S.xz, 1)
-    for op in PRE:
+    for op in (() if "x" in PRE else ("x",)) + PRE:
         what, i = op[0], int(op[1:] or 0)
-        if what == "z":
-            V.memset(T.tab[:, FV[i]:FV[i + 1]], 0.0).then_inc(S.vz, 1)
+        if what == "x":
+            V.memset(T.xb[:, 0:4 * Z], 0.0).then_inc(S.xz, 1)
+        elif what == "z":
+            V.memset(T.tab[:, FV[i]:FV[i + 1]], 0.0).then_inc(S.vz if i > 1 else S.dm1, 1)
         elif what == "h":
-            V.wait_ge(S.hr, 1)
+            V.wait_ge(S.hr, 1 if "v1" in PRE else 2)
             V.transpose(T.hc[:], T.hr[:]).then_inc(S.hc, 1)
         elif what == "v":
             V.wait_ge(S.lw, 1)
             V.wait_ge(S.hc, 1)
             V.tensor_scalar(T.vals[:, HC * i:HC * i + HC], T.lw[:], T.hc[:, 32 * i:32 * i + 1], None,
-                            A.max).then_inc(S.va, 1)
+                            A.max).then_inc(S["va%d" % i], 1)
         elif what == "k":
             V.wait_ge(S.kyl, 64)
             V.tensor_scalar(T.ka[:, 0:16], T.kr[:, 0:16], DW - 1, None, A.bitwise_and).then_inc(S.ka, 1)
         elif what == "l":
-            V.wait_ge(S.lkl, 128)
-            V.tensor_scalar(T.ka[:, 16:48], T.kr[:, 16:48], DW - 1, None, A.bitwise_and).then_inc(S.la, 1)
+            V.wait_ge(S.lkl, 64 * NL)
+            c = 16 + 16 * NL
+            if "d0" in SEQY:
+                V.wait_ge(S.dup, 16)
+                c = 48
+            V.tensor_scalar(T.ka[:, 16:c], T.kr[:, 16:c], DW - 1, None, A.bitwise_and).then_inc(S.la, 1)
         elif what == "b":
             V.wait_ge(S.kyl, 64)
-            V.wait_ge(S.lkl, 128)
-            V.tensor_scalar(T.ka[:], T.kr[:], DW - 1, None, A.bitwise_and).then_inc(S.ka, 1)
+            V.wait_ge(S.lkl, 64 * NL)
+            c = 16 + 16 * NL
+            V.tensor_scalar(T.ka[:, 0:c], T.kr[:, 0:c], DW - 1, None, A.bitwise_and).then_inc(S.ka, 1)
+        elif what == "D":
+            V.wait_ge(S.ka if "b" in PRE else S.la, 1)
+            c = 16 + 16 * i
+            V.tensor_copy(T.ko[:, c:c + 16 * NL], T.ka[:, 16:16 + 16 * NL]).then_inc(S.lf, 1)
         elif what == "K":
             V.wait_ge(S.ka, 1)
-            V.tensor_copy(T.ko[:], T.ka[:, 0:16]).then_inc(S.ko, 1)
+            V.tensor_copy(T.ko[:, 0:16], T.ka[:, 0:16]).then_inc(S.ko, 1)
         elif what == "d":
             V.wait_ge(S.ka if "b" in PRE else S.la, 1)
             V.tensor_copy(T.lf[:], T.ka[:, 16:48]).then_inc(S.lf, 1)
@@ -189,12 +222,15 @@ def rank_program(g, core, T, topo):
         elif what == "T":
             V.wait_ge(S.ka if "b" in PRE else S.la, 1)
             V.transpose(T.li[:], T.ka[:, 16:48]).then_inc(S.lt, 1)
-        elif what == "D":
-            V.wait_ge(S.la, 1)
-            V.tensor_copy(T.lu[:], T.ka[:, 16:48]).then_inc(S.lf, 1)
+        elif what == "B":
+            V.wait_ge(S.ka, 1)
+            c = 16 + 16 * NL
+            V.tensor_copy(T.ko[:, 0:c], T.ka[:, 0:c]).then_inc(S.ko, 1)
         elif what == "U":
-            V.wait_ge(S.lf, 1)
-            V.transpose(T.lO[:], T.lu[:]).then_inc(S.lo, 1)
+            V.wait_ge(S.ko, 1)
+            if "D0" in PRE or "D1" in PRE:
+                V.wait_ge(S.lf, sum(o[0] == "D" for o in PRE))
+            V.transpose(T.lO[:], T.ko[:, 16:48]).then_inc(S.lo, 1)
         elif what == "M":
             V.wait_ge(S.lt, 1)
             V.tensor_copy(T.lO[:], T.li[:]).then_inc(S.lo, 1)
@@ -208,18 +244,20 @@ def rank_program(g, core, T, topo):
             V.quantize_mx(T.wq[:], T.ws[:], T.wt[:]).then_inc(S.wqs, 1)
         elif i == 0:
             V.wait_ge(S.dm0, 1)
-            V.wait_ge(S.vz, len(FV) - 2)
+            V.wait_ge(S.dm1, 1)
+            V.wait_ge(S.vz, len(FV) - 3)
             if FD[-1] < DW:
                 V.wait_ge(S.gz, 1)
             V.wait_ge(S.sz, len(FS) - 1)
             if len(FD) > 1:
                 V.wait_ge(S.dz, 16 * (len(FD) - 1))
             V.wait_ge(S.ko, 1)
-            V.wait_ge(S.va, 2)
+            V.wait_ge(S.va0, 1)
             V.tensor_copy(T.tab[:, 0:DW].indirect(T.ko[:, 0:16]), T.vals[:, 0:HC]).then_inc(S.sc, 1)
         else:
             V.wait_ge(S.kar, par_n // KP)
             V.wait_ge(S.sc, 1)
+            V.wait_ge(S.va1, 1)
             V.tensor_copy(T.tab[:, 0:DW].indirect(T.kp[:, 0:16]), T.vals[:, HC:2 * HC]).then_inc(S.tabs, 1)
 
     first = [1]
@@ -247,7 +285,7 @@ def rank_program(g, core, T, topo):
             V.tensor_copy(T["q" + n][:, a:b].bitcast(dt.uint32),
                           T.pq[:, 0:WIN].bitcast(dt.uint32).indirect(of[:, a // 16:b // 16])).then_inc(S["pc" + op[1:]], 1)
             continue
-        if done[n]:
+        if done[n] and what != "b":
             V.wait_ge(S["v" + n], done[n])
         if what == "g":
             asked(V, n)
@@ -256,6 +294,10 @@ def rank_program(g, core, T, topo):
         elif what == "t":
             V.wait_ge(S["g" + n], 1)
             calls = [V.transpose(tur[:], row[:])]
+        elif what in "ab":
+            h = "ab".index(what)
+            V.wait_ge(S["g" + n + what], 1)
+            calls = [V.transpose(tur[:, HC * h:HC * h + HC], row[:, HC * h:HC * h + HC])]
         elif what == "s":
             V.wait_ge(S.cap, 1)
             calls = [V.tensor_tensor_scan(su[:, 64 * d:64 * d + 64], T.cap[:], tur[:, 0:512:8], 0.0, A.min, A.add)
@@ -274,15 +316,21 @@ def rank_program(g, core, T, topo):
 
     SC.wait_ge(S.dm0, 1)
     for a, b in zip(FS, FS[1:]):
+        if b - a > FV[1]:
+            SC.wait_ge(S.dm1, 1)
         SC.activation(T.tab[:, a:b], T.tab[:, 0:b - a], F.Copy).then_inc(S.sz, 1)
+    if "v1" not in PRE:
+        SC.wait_ge(S.va0, 1)
+        SC.activation(T.vals[:, HC:2 * HC], T.vals[:, 0:HC], F.Identity, bias=T.hc[:, 32:33]).then_inc(S.va1, 1)
     first = [1]
     for op in SEQS:
         what, n = op[0], op[1]
         if what == "g":
             asked(SC, n)
             a = GV["RO".index(n)] if "g" + n in SEQV else 0
-            SC.activation(T["row" + n][:, 16 * a:512], T.tab[:, 0:DW].indirect(T["l" + n][:, a:32]),
-                          F.Copy).then_inc(S["g" + n], 1)
+            a, b = {"": (a, 32), "a": (a, 16), "b": (16, 32)}[op[2:]]
+            SC.activation(T["row" + n][:, 16 * a:16 * b], T.tab[:, 0:DW].indirect(T["l" + n][:, a:b]),
+                          F.Copy).then_inc(S[op], 1)
         elif what == "y":
             SC.wait_ge(S["mm" + op[1:]], 1)
             SC.activation(*result(op), F.Copy).then_inc(S["cp" + op[1:]], 1)

from concourse.bass import DstId, RemoteDMATransfer
from concourse.mybir import dt, AluOpType as A, ActivationFunctionType as F

C8 = "float8_e4m3fn_x4"
Z, TC, HC = 16, 512, 256
DW = 8192
WIN = Z + 2 * TC
XCUT = (0, 256, 512)
SEQX = ("c0", "c1", "s01")
CUT = (0, 160, 352, 512)
CUTR = (0, 160, 352, 512)
FV = (0, 640, 1792, 1920, 2944, 3968)
FS = (3968, 4608, 6272)
FD = (6272, 6912, 7936)
PRE = ("z1", "h", "z2", "k", "x", "v0", "K", "z3", "l", "z4", "D0", "D1", "q0", "U", "s0", "q1", "s1")
SEQV = ("gR", "gO", "tR", "aO", "sR", "bO", "uR", "sO", "pR0", "uO", "pR1", "w-", "pO0", "pR2", "pO1", "pO2", "y00", "y01", "y02")
SEQS = ("gR", "gOa", "gOb", "pR0", "pR1", "pR2", "pO0", "pO1", "pO2", "y10", "y11", "y12")
SEQT = ("o0", "a0", "o1", "a1", "o2", "a2")
SEQG = ("c0", "s0", "c1", "s12", "c2")
SEQY = ("x0", "l0", "l1", "z0", "z1", "x1", "w0", "Y00", "Y10", "Y01", "Y11", "Y02", "Y12")
WW = "tabs"
CAPL = 1
NL = 1
KP = 2
GV = (16, 8)

SCRATCH = {
    "kr": ("sbuf", [128, 48], "int32"), "ka": ("sbuf", [128, 48], "int32"),
    "ko": ("sbuf", [128, 48], "uint16"), "kp": ("sbuf", [128, 16], "uint16"),
    "lf": ("sbuf", [128, 32], "float32"), "lt": ("sbuf", [128, 32], "float32"),
    "li": ("sbuf", [128, 32], "int32"), "lu": ("sbuf", [128, 32], "uint16"),
    "lO": ("sbuf", [128, 32], "uint16"), "lR": ("sbuf", [128, 32], "uint16"),
    "hr": ("sbuf", [128, 64], "bfloat16"), "hc": ("sbuf", [128, 64], "bfloat16"), "cap": ("sbuf", [128, 64], "float32"),
    "lw": ("sbuf", [128, 256], "bfloat16"),
    "vals": ("sbuf", [128, 512], "bfloat16"),
    "tab": ("sbuf", [128, DW], "bfloat16"),
    "xb": ("sbuf", [128, 4 * (Z + TC)], "bfloat16"), "wt": ("sbuf", [128, 1024], "bfloat16"),
    "wq": ("sbuf", [128, 256], C8), "ws": ("sbuf", [128, 256], "uint8"),
    "pq": ("sbuf", [128, WIN], C8), "ps": ("sbuf", [128, WIN], "uint8"),
    "qR": ("sbuf", [128, TC], C8), "sR": ("sbuf", [128, TC], "uint8"),
    "qO": ("sbuf", [128, TC], C8), "sO": ("sbuf", [128, TC], "uint8"),
    "aq": ("sbuf", [128, TC], C8), "as8": ("sbuf", [128, TC], "uint8"),
    "ysb": ("sbuf", [128, 1024], "float32"),
    "acc": ("psum", [128, 4096], "float32"),
}
for _n in "RO":
    SCRATCH["row" + _n] = ("sbuf", [128, 512], "bfloat16")
    SCRATCH["tur" + _n] = ("sbuf", [128, 512], "bfloat16")
    SCRATCH["su" + _n] = ("sbuf", [128, 128], "float32" if "c" + _n in SEQV else "uint16")
    SCRATCH["st" + _n] = ("sbuf", [128, 32], "float32")
    SCRATCH["of" + _n] = ("sbuf", [128, 32], "uint16")

NP = len(CUT) - 1
SEMAPHORES = ["dup", "dm1", "gOa", "gOb", "kyl", "lkl", "wl", "hr", "hc", "lw", "cap", "va0", "va1", "gz", "xz", "dm0", "vz", "sz", "dz", "ka", "la", "lf",
              "lt", "sc", "wqs", "ko", "lo", "kar", "rl", "tabs", "p1", "st0", "st1", "sent", "xl0", "xl1", "xl2", "q0", "q1", "q2"] + [
              s + n for s in ("g", "v", "of") for n in "RO"] + [
              s + str(j) for s in ("pcO", "psO", "mm0", "mm1", "cp0", "cp1") for j in range(NP)] + [
              s + str(j) for s in ("pcR", "psR") for j in range(len(CUTR) - 1)] + ["ar" + op for op in SEQG]


def rank_program(g, core, T, topo):
    rank = T.rank_of(core)
    if rank is None:
        return
    order = sorted(range(len(T.cores)), key=lambda r: (topo.die(T.cores[r]), r))
    k = order.index(rank)
    partner, mate = T.cores[order[(k + 2) % 4]], T.cores[order[k - k % 2 + 1 - k % 2]]
    S = T.sem
    V, SC, SY, TE = g.vector, g.scalar, g.sync, g.tensor
    sent = [0]

    def send(out, in_, sem, dst, part=0, parts=1):
        rid, pid, _ = topo.addr(dst)
        e = topo.engines(core, dst)
        n = len(e) // parts
        g.remote_dma(out, in_, S[sem], S.sent, pid, rid, sum(1 << q for q in e[part * n:part * n + n]))
        sent[0] += n

    def store(q, op, sem):
        o, j = int(op[1]), int(op[2])
        a, b = TC * o + CUT[j], TC * o + CUT[j + 1]
        q.wait_ge(S["cp" + op[1:]], 1)
        q.dma_start(T.y[:, a:b], T.ysb[:, a:b]).then_inc(sem, 16)

    def result(op):
        o, j = int(op[1]), int(op[2])
        a, n = 1024 * j + 512 * o, CUT[j + 1] - CUT[j]
        return T.ysb[:, TC * o + CUT[j]:TC * o + CUT[j + 1]], T.acc[:, a:a + n]

    par_n, mate_n = len(topo.engines(partner, core)), len(topo.engines(mate, core))

    own, par = Z, Z + TC
    for c, src, sem in ((0, T.ky, S.kyl), (16, T.lk, S.lkl), (32, T.lk, S.lkl))[:1 + NL]:
        for q, u in ((SY, 0), (SC, 1)):
            for j in range(2):
                p = 32 * (2 * j + u)
                if c == 0 or (u and c == 16) or "l0" not in SEQY:
                    q.dma_start(T.kr[p:p + 32, c:c + 16], src[:]).then_inc(sem, 16)
    for op in SEQY:
        what, i = op[0], int(op[1])
        if what == "l":
            SY.dma_start(T.kr[64 * i:64 * i + 32, 16:32], T.lk[:]).then_inc(S.lkl, 16)
        elif what == "m":
            SY.dma_start(T.kr[32 * i:32 * i + 32, 32:48], T.lk[:]).then_inc(S.lkl, 16)
        elif what == "x":
            a, b = 4 * XCUT[i], 4 * XCUT[i + 1]
            SY.dma_start(T.xb[:, 4 * Z + a:4 * Z + b], T.x[:, a:b]).then_inc(S["xl%d" % i], 16)
        elif what == "z":
            SY.wait_ge(S.dm0, 1)
            if FD[i + 1] - FD[i] > FV[1]:
                SY.wait_ge(S.dm1, 1)
            SY.dma_start(T.tab[:, FD[i]:FD[i + 1]], T.tab[:, 0:FD[i + 1] - FD[i]]).then_inc(S.dz, 16)
        elif what == "d":
            SY.wait_ge(S.lkl, 64)
            SY.dma_start(T.kr[:, 32:48], T.kr[:, 16:32]).then_inc(S.dup, 16)
        elif what == "w":
            SY.wait_ge(S[WW], 1)
            SY.dma_start(T.wt[:], T.w[:]).then_inc(S.wl, 16)
        else:
            store(SY, op, S.st0)
    SY.wait_ge(S.st0, 16 * sum(op[0] == "Y" for op in SEQY))

    def iota(out, pattern, base, sem):
        g.iota(out, pattern, base, 0, allow_small_or_imprecise_dtypes=True).then_inc(S[sem], 1)

    if "v1" in PRE:
        iota(T.hr[:], [[TC, 2], [8, 2], [256, 16]], Z + 256 - 8 * 256, "hr")
    else:
        iota(T.hr[:, 0:32], [[8, 2], [256, 16]], Z + 256 - 8 * 256, "hr")
        iota(T.hr[:, 32:64], [[0, 2], [TC // 8, 16]], 0, "hr")
    iota(T.lw[:], [[16, 16], [1, 8], [256, 2]], -256, "lw")
    if not CAPL:
        iota(T.cap[:], [[0, 16], [2048, 4]], 0, "cap")
    if FD[-1] < DW:
        iota(T.tab[:, FD[-1]:DW], [[0, DW - FD[-1]]], 0, "gz")
    g.wait_ge(S.ko, 1)
    send(T.kp[:], T.ko[:, 0:16], "kar", partner, 0, KP)
    g.wait_ge(S.lo, 1)
    send(T.lR[:], T.lO[:], "rl", mate, KP - 1, KP)
    if CAPL:
        iota(T.cap[:], [[0, 16], [2048, 4]], 0, "cap")
    for op in SEQX:
        a, b = XCUT[int(op[1])], XCUT[int(op[-1]) + 1]
        for h in op[1:]:
            g.wait_ge(S["q" + h], 1)
        if op[0] == "c":
            send(T.pq[:, par + a:par + b].bitcast(dt.uint8), T.pq[:, own + a:own + b].bitcast(dt.uint8), "p1", partner)
        else:
            send(T.ps[:, par + a:par + b], T.ps[:, own + a:own + b], "p1", partner)
    for op in SEQG:
        a, b = CUTR[int(op[1])], CUTR[int(op[-1]) + 1]
        for j in op[1:]:
            g.wait_ge(S["p%sR%s" % (op[0], j)], 1)
        if op[0] == "c":
            send(T.aq[:, a:b].bitcast(dt.uint8), T.qR[:, a:b].bitcast(dt.uint8), "ar" + op, mate)
        else:
            send(T.as8[:, a:b], T.sR[:, a:b], "ar" + op, mate)
    g.wait_ge(S.sent, sent[0])

    def window(q):
        for h in range(len(XCUT) - 1):
            q.wait_ge(S["q%d" % h], 1)
        q.wait_ge(S.p1, len(SEQX) * par_n)

    def asked(q, n):
        q.wait_ge(S.tabs, 1)
        if n == "R":
            q.wait_ge(S.rl, mate_n // KP)
        else:
            q.wait_ge(S.lo, 1)

    def quantise(i):
        V.wait_ge(S["xl%d" % i], 16)
        if i == 0:
            V.wait_ge(S.xz, 1)
        a, b = (own + XCUT[i] if i else 0), own + XCUT[i + 1]
        V.quantize_mx(T.pq[:, a:b], T.ps[:, a:b], T.xb[:, 4 * a:4 * b]).then_inc(S["q%d" % i], 1)

    V.memset(T.tab[:, FV[0]:FV[1]], 0.0).then_inc(S.dm0, 1)
    for op in (() if "x" in PRE else ("x",)) + PRE:
        what, i = op[0], int(op[1:] or 0)
        if what == "x":
            V.memset(T.xb[:, 0:4 * Z], 0.0).then_inc(S.xz, 1)
        elif what == "z":
            V.memset(T.tab[:, FV[i]:FV[i + 1]], 0.0).then_inc(S.vz if i > 1 else S.dm1, 1)
        elif what == "h":
            V.wait_ge(S.hr, 1 if "v1" in PRE else 2)
            V.transpose(T.hc[:], T.hr[:]).then_inc(S.hc, 1)
        elif what == "v":
            V.wait_ge(S.lw, 1)
            V.wait_ge(S.hc, 1)
            V.tensor_scalar(T.vals[:, HC * i:HC * i + HC], T.lw[:], T.hc[:, 32 * i:32 * i + 1], None,
                            A.max).then_inc(S["va%d" % i], 1)
        elif what == "k":
            V.wait_ge(S.kyl, 64)
            V.tensor_scalar(T.ka[:, 0:16], T.kr[:, 0:16], DW - 1, None, A.bitwise_and).then_inc(S.ka, 1)
        elif what == "l":
            V.wait_ge(S.lkl, 64 * NL)
            c = 16 + 16 * NL
            if "d0" in SEQY:
                V.wait_ge(S.dup, 16)
                c = 48
            V.tensor_scalar(T.ka[:, 16:c], T.kr[:, 16:c], DW - 1, None, A.bitwise_and).then_inc(S.la, 1)
        elif what == "b":
            V.wait_ge(S.kyl, 64)
            V.wait_ge(S.lkl, 64 * NL)
            c = 16 + 16 * NL
            V.tensor_scalar(T.ka[:, 0:c], T.kr[:, 0:c], DW - 1, None, A.bitwise_and).then_inc(S.ka, 1)
        elif what == "D":
            V.wait_ge(S.ka if "b" in PRE else S.la, 1)
            c = 16 + 16 * i
            V.tensor_copy(T.ko[:, c:c + 16 * NL], T.ka[:, 16:16 + 16 * NL]).then_inc(S.lf, 1)
        elif what == "K":
            V.wait_ge(S.ka, 1)
            V.tensor_copy(T.ko[:, 0:16], T.ka[:, 0:16]).then_inc(S.ko, 1)
        elif what == "d":
            V.wait_ge(S.ka if "b" in PRE else S.la, 1)
            V.tensor_copy(T.lf[:], T.ka[:, 16:48]).then_inc(S.lf, 1)
        elif what == "t":
            V.wait_ge(S.lf, 1)
            V.transpose(T.lt[:], T.lf[:]).then_inc(S.lt, 1)
        elif what == "T":
            V.wait_ge(S.ka if "b" in PRE else S.la, 1)
            V.transpose(T.li[:], T.ka[:, 16:48]).then_inc(S.lt, 1)
        elif what == "B":
            V.wait_ge(S.ka, 1)
            c = 16 + 16 * NL
            V.tensor_copy(T.ko[:, 0:c], T.ka[:, 0:c]).then_inc(S.ko, 1)
        elif what == "U":
            V.wait_ge(S.ko, 1)
            if "D0" in PRE or "D1" in PRE:
                V.wait_ge(S.lf, sum(o[0] == "D" for o in PRE))
            V.transpose(T.lO[:], T.ko[:, 16:48]).then_inc(S.lo, 1)
        elif what == "M":
            V.wait_ge(S.lt, 1)
            V.tensor_copy(T.lO[:], T.li[:]).then_inc(S.lo, 1)
        elif what == "L":
            V.wait_ge(S.lt, 1)
            V.tensor_copy(T.lO[:], T.lt[:]).then_inc(S.lo, 1)
        elif what == "q":
            quantise(i)
        elif what == "w":
            V.wait_ge(S.wl, 16)
            V.quantize_mx(T.wq[:], T.ws[:], T.wt[:]).then_inc(S.wqs, 1)
        elif i == 0:
            V.wait_ge(S.dm0, 1)
            V.wait_ge(S.dm1, 1)
            V.wait_ge(S.vz, len(FV) - 3)
            if FD[-1] < DW:
                V.wait_ge(S.gz, 1)
            V.wait_ge(S.sz, len(FS) - 1)
            if len(FD) > 1:
                V.wait_ge(S.dz, 16 * (len(FD) - 1))
            V.wait_ge(S.ko, 1)
            V.wait_ge(S.va0, 1)
            V.tensor_copy(T.tab[:, 0:DW].indirect(T.ko[:, 0:16]), T.vals[:, 0:HC]).then_inc(S.sc, 1)
        else:
            V.wait_ge(S.kar, par_n // KP)
            V.wait_ge(S.sc, 1)
            V.wait_ge(S.va1, 1)
            V.tensor_copy(T.tab[:, 0:DW].indirect(T.kp[:, 0:16]), T.vals[:, HC:2 * HC]).then_inc(S.tabs, 1)

    first = [1]
    done = {"R": 0, "O": 0}
    for op in SEQV:
        what, n = op[0], op[1]
        if what == "w":
            V.wait_ge(S.wl, 16)
            V.quantize_mx(T.wq[:], T.ws[:], T.wt[:]).then_inc(S.wqs, 1)
            continue
        if what == "q":
            quantise(int(n))
            continue
        if what == "y":
            V.wait_ge(S["mm" + op[1:]], 1)
            V.tensor_copy(*result(op)).then_inc(S["cp" + op[1:]], 1)
            continue
        row, tur, su, st, of = (T[b + n] for b in ("row", "tur", "su", "st", "of"))
        if what == "p":
            if first[0]:
                window(V)
                first[0] = 0
            V.wait_ge(S["of" + n], 1)
            a, b = (CUTR if n == "R" else CUT)[int(op[2]):int(op[2]) + 2]
            V.tensor_copy(T["q" + n][:, a:b].bitcast(dt.uint32),
                          T.pq[:, 0:WIN].bitcast(dt.uint32).indirect(of[:, a // 16:b // 16])).then_inc(S["pc" + op[1:]], 1)
            continue
        if done[n] and what != "b":
            V.wait_ge(S["v" + n], done[n])
        if what == "g":
            asked(V, n)
            c = GV["RO".index(n)]
            calls = [V.tensor_copy(row[:, 0:16 * c], T.tab[:, 0:DW].indirect(T["l" + n][:, 0:c]))]
        elif what == "t":
            V.wait_ge(S["g" + n], 1)
            calls = [V.transpose(tur[:], row[:])]
        elif what in "ab":
            h = "ab".index(what)
            V.wait_ge(S["g" + n + what], 1)
            calls = [V.transpose(tur[:, HC * h:HC * h + HC], row[:, HC * h:HC * h + HC])]
        elif what == "s":
            V.wait_ge(S.cap, 1)
            calls = [V.tensor_tensor_scan(su[:, 64 * d:64 * d + 64], T.cap[:], tur[:, 0:512:8], 0.0, A.min, A.add)
                     for d in range(2)]
        elif what == "u" and "c" + n in SEQV:
            calls = [V.transpose(st[:], su[:, 3:128:4])]
        elif what == "u":
            V.transpose(of[:], su[:, 3:128:4]).then_inc(S["of" + n], 1)
            continue
        else:
            V.tensor_copy(of[:], st[:]).then_inc(S["of" + n], 1)
            continue
        for ins in calls:
            ins.then_inc(S["v" + n], 1)
        done[n] += len(calls)

    SC.wait_ge(S.dm0, 1)
    for a, b in zip(FS, FS[1:]):
        if b - a > FV[1]:
            SC.wait_ge(S.dm1, 1)
        SC.activation(T.tab[:, a:b], T.tab[:, 0:b - a], F.Copy).then_inc(S.sz, 1)
    if "v1" not in PRE:
        SC.wait_ge(S.va0, 1)
        SC.activation(T.vals[:, HC:2 * HC], T.vals[:, 0:HC], F.Identity, bias=T.hc[:, 32:33]).then_inc(S.va1, 1)
    first = [1]
    for op in SEQS:
        what, n = op[0], op[1]
        if what == "g":
            asked(SC, n)
            a = GV["RO".index(n)] if "g" + n in SEQV else 0
            a, b = {"": (a, 32), "a": (a, 16), "b": (16, 32)}[op[2:]]
            SC.activation(T["row" + n][:, 16 * a:16 * b], T.tab[:, 0:DW].indirect(T["l" + n][:, a:b]),
                          F.Copy).then_inc(S[op], 1)
        elif what == "y":
            SC.wait_ge(S["mm" + op[1:]], 1)
            SC.activation(*result(op), F.Copy).then_inc(S["cp" + op[1:]], 1)
        elif what == "Y":
            store(SC, op, S.st1)
        else:
            if first[0]:
                window(SC)
                first[0] = 0
            SC.wait_ge(S["of" + n], 1)
            a, b = (CUTR if n == "R" else CUT)[int(op[2]):int(op[2]) + 2]
            SC.activation(T["s" + n][:, a:b], T.ps[:, 0:WIN].indirect(T["of" + n][:, a // 16:b // 16]),
                          F.Copy).then_inc(S["ps" + op[1:]], 1)
    if any(op[0] == "Y" for op in SEQS):
        SC.wait_ge(S.st1, 16 * sum(op[0] == "Y" for op in SEQS))

    TE.wait_ge(S.wqs, 1)
    begun = []
    for op in SEQT:
        j = int(op[1])
        a, b = CUT[j], CUT[j + 1]
        begin = j not in begun
        begun.append(j)
        if op[0] == "o":
            q, s = T.qO, T.sO
            TE.wait_ge(S["pcO%d" % j], 1)
            TE.wait_ge(S["psO%d" % j], 1)
        else:
            q, s = T.aq, T.as8
            for sent_op in SEQG:
                if CUTR[int(sent_op[1])] < b and a < CUTR[int(sent_op[-1]) + 1]:
                    TE.wait_ge(S["ar" + sent_op], mate_n)
        for o in range(2):
            c = 1024 * j + 512 * o
            ins = TE.matmul_mx(T.acc[:, c:c + b - a], T.wq[:, 128 * o:128 * o + 128], T.ws[:, 128 * o:128 * o + 128],
                               q[:, a:b], s[:, a:b], begin, not begin)
            if not begin:
                ins.then_inc(S["mm%d%d" % (o, j)], 1)
